import numpy as np
import ml_dtypes


def mxq(x, axis, fmt="e4m3"):
    dtype, down = {"e4m3": (ml_dtypes.float8_e4m3fn, 7), "e5m2": (ml_dtypes.float8_e5m2, 14)}[fmt]
    v = np.moveaxis(np.asarray(x, np.float32).astype(ml_dtypes.bfloat16).astype(np.float64), axis, -1)
    blocks = v.reshape(v.shape[:-1] + (-1, 32))
    amax = np.abs(blocks).max(-1, keepdims=True)
    byte = np.maximum(np.where(amax > 0, np.frexp(amax)[1] - 1 + 127, 0) - down, 1)
    scale = np.exp2(byte - 127.0)
    codes = (blocks / scale).astype(np.float32).astype(dtype).astype(np.float64)
    return np.moveaxis((codes * scale).reshape(v.shape), -1, axis)


WIDE = False


def mx_kscale(k):
    if not WIDE:
        return np.ones(k)
    levels = np.array([10, -10, 5, -5, 0])
    if k % 512:
        return np.exp2(np.random.permutation(np.resize(levels, k // 32))).repeat(32)
    a = np.empty((k // 512, 16))
    for p in range(k // 512):
        a[p, :8] = np.random.permutation(np.resize(levels, 8))
        for g in range(8):
            far = levels[np.abs(levels - a[p, g]) >= 10]
            a[p, g + 8] = far[np.random.randint(len(far))]
    return np.exp2(a.ravel()).repeat(32)


def f64(x):
    return np.asarray(x).astype(np.float64)


def striped(idx):
    return np.tile(np.asarray(idx).reshape(-1, 16).T, (8, 1)).astype(np.uint16)


def unstriped(offs):
    return offs[:16].T.reshape(-1).astype(np.int64)


def striped8(idx):
    return np.asarray(idx).reshape(8, -1, 16).transpose(0, 2, 1).reshape(128, -1).astype(np.uint16)


def unstriped8(offs):
    return offs.reshape(8, 16, -1).transpose(0, 2, 1).reshape(8, -1).astype(np.int64)


def pick8(x, idx, run):
    r = np.arange(len(x))
    return x[r[:, None], idx[r % (8 * run) // run]]


E2M1 = np.array([0.0, 0.5, 1.0, 1.5, 2.0, 3.0, 4.0, 6.0, -0.0, -0.5, -1.0, -1.5, -2.0, -3.0, -4.0, -6.0])


def pack_weight(w, fmt):
    k, n = w.shape
    w = f64(np.asarray(w, np.float32).astype(ml_dtypes.bfloat16)).reshape(k // 32, 32, n)
    amax = np.abs(w).max(1)
    if fmt == "e4m3":
        byte = np.frexp(amax)[1] - 1 + 127 - 7
    else:
        mant, ex = np.frexp(amax / 6.0)
        byte = np.where(mant > 0.5, ex, ex - 1) + 127
    byte = np.clip(np.where(amax > 0, byte, 1), 1, 254)
    scaled = (w * np.exp2(127.0 - byte)[:, None, :]).reshape(k, n).astype(np.float32)
    by_word = np.ascontiguousarray(scaled.reshape(k // 512, 128, 4, n).transpose(0, 1, 3, 2))
    if fmt == "e4m3":
        words = by_word.astype(ml_dtypes.float8_e4m3fn).view(np.uint8)
    else:
        c = by_word.astype(ml_dtypes.float4_e2m1fn).view(np.uint8) & 0xF
        words = (c[..., 0::2] | (c[..., 1::2] << 4)).reshape(k // 512, 128, 2 * n)
    return np.ascontiguousarray(words), np.ascontiguousarray(byte.astype(np.uint8).reshape(k // 512, 16, n))


def unpack_weight(words, scales, fmt):
    g, _, n = scales.shape
    words = np.ascontiguousarray(words).reshape(g, 128, n, -1)
    if fmt == "e4m3":
        vals = words.view(ml_dtypes.float8_e4m3fn).astype(np.float64)
    else:
        nib = np.empty((g, 128, n, 4), np.uint8)
        nib[..., 0::2] = words & 0xF
        nib[..., 1::2] = words >> 4
        vals = E2M1[nib]
    vals = vals * np.repeat(np.exp2(scales.astype(np.float64) - 127.0), 8, axis=1)[..., None]
    return vals.transpose(0, 1, 3, 2).reshape(g * 512, n)


K, J, R, T, F, O, S, C, N = 512, 512, 512, 2048, 1024, 256, 256, 512, 256


def setup_inputs():
    n = np.random.standard_normal
    idx = np.random.permutation(T)[:J]
    idx2 = np.random.permutation(F)[:R]
    idx3 = np.stack([np.random.permutation(J)[:S] for _ in range(8)])
    idx4 = np.stack([np.random.permutation(J)[:S] for _ in range(8)])
    idx5 = np.stack([np.random.permutation(C)[:S] for _ in range(8)])
    idx6 = np.stack([np.random.permutation(C)[:S] for _ in range(8)])
    idx7 = np.stack([np.random.permutation(C)[:O] for _ in range(8)])
    fk = mx_kscale(K)
    fr = mx_kscale(R)
    tr = np.ones(F)
    tr[idx2] = fr
    xtp = pack_weight(n((K, T)) * fk[:, None], "e2m1")
    wtp = pack_weight(n((K, F)) * 1 / np.sqrt(K) / fk[:, None] * tr, "e4m3")
    wbp = pack_weight(n((R, N)) * 1 / np.sqrt(R) / fr[:, None], "e2m1")
    return {
        "xt_words": xtp[0],
        "xt_scales": xtp[1],
        "wt_words": wtp[0],
        "wt_scales": wtp[1],
        "sa": (np.random.uniform(0.5, 1.6, (R, 1))).astype(np.float32),
        "sb": (np.random.uniform(0.5, 1.6, (R, 1))).astype(np.float32),
        "sd": (np.random.uniform(0.5, 1.6, (R, 1))).astype(np.float32),
        "wb_words": wbp[0],
        "wb_scales": wbp[1],
        "offs": striped(idx),
        "offs2": striped(idx2),
        "offs3": striped8(idx3),
        "offs4": striped8(idx4),
        "offs5": striped8(idx5),
        "offs6": striped8(idx6),
        "offs7": striped8(idx7),
    }


def reference(xt_words, xt_scales, wt_words, wt_scales, sa, sb, sd, wb_words, wb_scales, offs, offs2, offs3, offs4, offs5, offs6, offs7):
    idx = unstriped(offs)
    idx2 = unstriped(offs2)
    idx3 = unstriped8(offs3)
    idx4 = unstriped8(offs4)
    idx5 = unstriped8(offs5)
    idx6 = unstriped8(offs6)
    idx7 = unstriped8(offs7)
    xtu = unpack_weight(xt_words, xt_scales, "e2m1")
    wtu = unpack_weight(wt_words, wt_scales, "e4m3")
    wbu = unpack_weight(wb_words, wb_scales, "e2m1")
    wtidx2g = wtu[:, idx2]
    xtidxg = xtu[:, idx]
    a = wtidx2g.T @ xtidxg
    h1 = pick8(a, idx3, 64) * f64(sa)
    h2 = pick8(a, idx4, 64) * f64(sb)
    pw = np.zeros((R, C))
    pw[np.arange(R)[:, None], idx5[np.arange(R) % 512 // 64]] = h1
    pv = np.zeros((R, C))
    pv[np.arange(R)[:, None], idx6[np.arange(R) % 512 // 64]] = h2
    g1 = np.abs(pw - pv)
    hid = pick8(g1, idx7, 64) * f64(sd)
    hidq = mxq(hid, 0, "e4m3")
    y = wbu.T @ hidq
    return y

@@ -1,0 +1,158 @@
+from contextlib import ExitStack
+
+import concourse.mybir as mybir
+
+K, J, R, T, F, O, S, C, N = 512, 512, 512, 2048, 1024, 256, 256, 512, 256
+FLOPS = 2 * K * R * J + 2 * R * N * O
+
+F32 = mybir.dt.float32
+BF16 = mybir.dt.bfloat16
+I32 = mybir.dt.int32
+U32 = mybir.dt.uint32
+U16 = mybir.dt.uint16
+U8 = mybir.dt.uint8
+FP8X4 = mybir.dt.float8_e4m3fn_x4
+FP4X4 = mybir.dt.float4_e2m1fn_x4
+COPY = mybir.ActivationFunctionType.Copy
+ALU = mybir.AluOpType
+
+P = 128
+PACK = 4
+LIST = 16
+HALF_J = J // 2
+HALF_O = O // 2
+
+
+def tile_picked_tokens_store_one_doublepost_one_plain_kernel(
+    tc, xt_words, xt_scales, wt_words, wt_scales, sa, sb, sd, wb_words, wb_scales,
+    offs, offs2, offs3, offs4, offs5, offs6, offs7, out,
+):
+    nc = tc.nc
+    with ExitStack() as ctx:
+        keep = ctx.enter_context(tc.tile_pool(name="keep", bufs=1))
+        psum = ctx.enter_context(tc.psum_pool(name="psum", bufs=1))
+
+        def load_list(name, src):
+            tile = keep.tile(list(src.shape), U16, name=name)
+            nc.sync.dma_start(tile[:], src)
+            return tile
+
+        def scale_tile(name, width):
+            tile = keep.tile([P, width], U8, name=name, align_bytes=64)
+            nc.vector.memset(tile[:].bitcast(I32), 0)
+            return tile
+
+        def load_scales(tile, src):
+            for q in range(4):
+                nc.sync.dma_start(
+                    tile[32 * q : 32 * q + 4, :].bitcast(I32),
+                    src[0, 4 * q : 4 * q + 4, :].bitcast(I32),
+                )
+
+        def load_row_weights(name, src):
+            tile = keep.tile([P, PACK], F32, name=name)
+            nc.sync.dma_start(tile[:], src.rearrange("(p t) o -> p (t o)", t=PACK))
+            return tile
+
+        wt_s = scale_tile("wt_s", F)
+        xt_s = scale_tile("xt_s", T)
+        wb_s = scale_tile("wb_s", N)
+
+        list2 = load_list("list2", offs2)
+        wt_w = keep.tile([P, F], U32, name="wt_w", align_bytes=64)
+        nc.sync.dma_start(wt_w[:].bitcast(I32), wt_words[0].rearrange("p f t -> p (f t)").bitcast(I32))
+        load_scales(wt_s, wt_scales)
+        list1 = load_list("list1", offs)
+        xt_w = keep.tile([P, T], U16, name="xt_w", align_bytes=64)
+        nc.sync.dma_start(xt_w[:].bitcast(I32), xt_words[0].bitcast(I32))
+        load_scales(xt_s, xt_scales)
+        list3 = load_list("list3", offs3)
+        sa_t = load_row_weights("sa_t", sa)
+        list4 = load_list("list4", offs4)
+        sb_t = load_row_weights("sb_t", sb)
+        list5 = load_list("list5", offs5)
+        list6 = load_list("list6", offs6)
+        list7 = load_list("list7", offs7)
+        sd_t = load_row_weights("sd_t", sd)
+        wb_w = keep.tile([P, 2 * N], U8, name="wb_w", align_bytes=64)
+        nc.sync.dma_start(wb_w[:].bitcast(I32), wb_words[0].bitcast(I32))
+        load_scales(wb_s, wb_scales)
+
+        wg_s = keep.tile([P, PACK, P], U8, name="wg_s", align_bytes=64)
+        wg_w = keep.tile([P, PACK, P], U32, name="wg_w", align_bytes=64)
+        nc.vector.tensor_copy(wg_w[:].rearrange("p t m -> p m t"), wt_w[:].indirect(list2[:]))
+        nc.vector.tensor_copy(wg_s[:].rearrange("p t m -> p m t"), wt_s[:].indirect(list2[:]))
+
+        xg_w = keep.tile([P, J], U16, name="xg_w", align_bytes=64)
+        xg_s = keep.tile([P, J], U8, name="xg_s", align_bytes=64)
+        nc.vector.tensor_copy(xg_w[:], xt_w[:].indirect(list1[:]))
+        for h in range(2):
+            cols = slice(h * HALF_J, (h + 1) * HALF_J)
+            entries = list1[:, h * HALF_J // LIST : (h + 1) * HALF_J // LIST]
+            nc.vector.tensor_copy(xg_s[:, cols], xt_s[:].indirect(entries))
+
+        def first_product(acc, t, cols):
+            nc.tensor.matmul_mx(
+                acc, lhsT=wg_w[:, t, :].bitcast(FP8X4), lhsT_scale=wg_s[:, t, :],
+                rhs=xg_w[:, cols].bitcast(FP4X4), rhs_scale=xg_s[:, cols], start=True, stop=True,
+            )
+
+        a = [keep.tile([P, J], F32, name=f"a{t}") for t in range(PACK)]
+        for i, (lo, hi) in enumerate([(0, HALF_J), (HALF_J, HALF_J + P), (HALF_J + P, J)]):
+            acc = psum.tile([P, hi - lo], F32, name="acc_first", tag=f"bank{i}")
+            first_product(acc[:], 0, slice(lo, hi))
+            if hi == J:
+                nc.vector.tensor_copy(a[0][:, lo:hi], acc[:])
+            else:
+                nc.scalar.activation(a[0][:, lo:hi], acc[:], COPY)
+        for t in range(1, PACK):
+            acc = psum.tile([P, J], F32, name=f"acc{t}")
+            first_product(acc[:], t, slice(0, J))
+            nc.vector.tensor_copy(a[t][:], acc[:])
+
+        g1 = []
+        for t in range(PACK):
+            h1 = keep.tile([P, S], F32, name="h1", tag="seats")
+            h2 = keep.tile([P, S], F32, name="h2")
+            pw = keep.tile([P, C], F32, name="pw", bufs=2)
+            pv = keep.tile([P, C], F32, name="pv", bufs=2)
+            nc.vector.memset(pw[:].bitcast(I32), 0)
+            nc.vector.memset(pv[:].bitcast(I32), 0)
+            nc.scalar.activation(h1[:], a[t][:].indirect(list3[:]), COPY, scale=sa_t[:, t : t + 1])
+            nc.scalar.activation(h2[:], a[t][:].indirect(list4[:]), COPY, scale=sb_t[:, t : t + 1])
+            nc.scalar.activation(pw[:].indirect(list5[:]), h1[:], COPY)
+            nc.scalar.activation(pv[:].indirect(list6[:]), h2[:], COPY)
+            diff = keep.tile([P, C], F32, name="diff", bufs=2)
+            g = keep.tile([P, C], F32, name=f"g1_{t}")
+            halves = [slice(0, C // 2), slice(C // 2, C)]
+            for cols in halves:
+                nc.vector.tensor_tensor(diff[:, cols], pw[:, cols], pv[:, cols], ALU.subtract)
+            for cols in halves:
+                nc.vector.scalar_tensor_tensor(g[:, cols], diff[:, cols], -1.0, diff[:, cols], ALU.mult, ALU.max)
+            g1.append(g)
+
+        hid = keep.tile([P, 2, PACK, HALF_O], BF16, name="hid", tag="seats")
+        out_rows = out.rearrange("(b p) o -> p b o", p=P)
+        for h in range(2):
+            entries = list7[:, h * HALF_O // LIST : (h + 1) * HALF_O // LIST]
+            for t in range(PACK):
+                nc.scalar.activation(hid[:, h, t, :], g1[t][:].indirect(entries), COPY, scale=sd_t[:, t : t + 1])
+            woven = keep.tile([P, HALF_O, PACK], BF16, name=f"woven{h}", align_bytes=64)
+            nc.vector.tensor_copy(woven[:], hid[:, h].rearrange("p t o -> p o t"))
+            hq_w = keep.tile([P, HALF_O], U32, name=f"hq_w{h}", align_bytes=64)
+            hq_s = keep.tile([P, HALF_O], U8, name=f"hq_s{h}", align_bytes=64)
+            nc.vector.quantize_mx(hq_w[:].bitcast(FP8X4), hq_s[:], woven[:].rearrange("p o t -> p (o t)"))
+            for b in range(N // P):
+                acc = psum.tile([P, HALF_O], F32, name="acc_out", tag=f"bank{2 * h + b}")
+                nc.tensor.matmul_mx(
+                    acc[:], lhsT=wb_w[:, 2 * P * b : 2 * P * (b + 1)].bitcast(FP4X4),
+                    lhsT_scale=wb_s[:, P * b : P * (b + 1)],
+                    rhs=hq_w[:].bitcast(FP8X4), rhs_scale=hq_s[:], start=True, stop=True,
+                )
+                y = keep.tile([P, HALF_O], F32, name=f"y{h}{b}")
+                if b == 0:
+                    nc.scalar.copy(y[:], acc[:])
+                    nc.scalar.dma_start(out_rows[:, b, h * HALF_O : (h + 1) * HALF_O], y[:])
+                else:
+                    nc.vector.tensor_copy(y[:], acc[:])
+                    nc.sync.dma_start(out_rows[:, b, h * HALF_O : (h + 1) * HALF_O], y[:])

@@ -38,7 +38,7 @@ def tile_picked_tokens_store_one_doublepost_one_plain_kernel(
             return tile
 
         def scale_tile(name, width):
-            tile = keep.tile([P, width], U8, name=name, align_bytes=64)
+            tile = keep.tile([P, width], U8, name=name, tag=name, align_bytes=64)
             nc.vector.memset(tile[:].bitcast(I32), 0)
             return tile
 
@@ -59,10 +59,10 @@ def tile_picked_tokens_store_one_doublepost_one_plain_kernel(
         wb_s = scale_tile("wb_s", N)
 
         list2 = load_list("list2", offs2)
+        list1 = load_list("list1", offs)
+        load_scales(wt_s, wt_scales)
         wt_w = keep.tile([P, F], U32, name="wt_w", align_bytes=64)
         nc.sync.dma_start(wt_w[:].bitcast(I32), wt_words[0].rearrange("p f t -> p (f t)").bitcast(I32))
-        load_scales(wt_s, wt_scales)
-        list1 = load_list("list1", offs)
         xt_w = keep.tile([P, T], U16, name="xt_w", align_bytes=64)
         nc.sync.dma_start(xt_w[:].bitcast(I32), xt_words[0].bitcast(I32))
         load_scales(xt_s, xt_scales)
@@ -79,9 +79,9 @@ def tile_picked_tokens_store_one_doublepost_one_plain_kernel(
         load_scales(wb_s, wb_scales)
 
         wg_s = keep.tile([P, PACK, P], U8, name="wg_s", align_bytes=64)
-        wg_w = keep.tile([P, PACK, P], U32, name="wg_w", align_bytes=64)
-        nc.vector.tensor_copy(wg_w[:].rearrange("p t m -> p m t"), wt_w[:].indirect(list2[:]))
+        wg_w = keep.tile([P, PACK, P], U32, name="wg_w", tag="wg_w", align_bytes=64)
         nc.vector.tensor_copy(wg_s[:].rearrange("p t m -> p m t"), wt_s[:].indirect(list2[:]))
+        nc.vector.tensor_copy(wg_w[:].rearrange("p t m -> p m t"), wt_w[:].indirect(list2[:]))
 
         xg_w = keep.tile([P, J], U16, name="xg_w", align_bytes=64)
         xg_s = keep.tile([P, J], U8, name="xg_s", align_bytes=64)
@@ -114,8 +114,8 @@ def tile_picked_tokens_store_one_doublepost_one_plain_kernel(
         for t in range(PACK):
             h1 = keep.tile([P, S], F32, name="h1", tag="seats")
             h2 = keep.tile([P, S], F32, name="h2")
-            pw = keep.tile([P, C], F32, name="pw", bufs=2)
-            pv = keep.tile([P, C], F32, name="pv", bufs=2)
+            pw = keep.tile([P, C], F32, name="pw", tag=("pw_even", "xt_s")[t % 2], align_bytes=64)
+            pv = keep.tile([P, C], F32, name="pv", tag=("pv_even", "wg_w")[t % 2], align_bytes=64)
             nc.vector.memset(pw[:].bitcast(I32), 0)
             nc.vector.memset(pv[:].bitcast(I32), 0)
             nc.scalar.activation(h1[:], a[t][:].indirect(list3[:]), COPY, scale=sa_t[:, t : t + 1])
@@ -138,7 +138,10 @@ def tile_picked_tokens_store_one_doublepost_one_plain_kernel(
             for t in range(PACK):
                 nc.scalar.activation(hid[:, h, t, :], g1[t][:].indirect(entries), COPY, scale=sd_t[:, t : t + 1])
             woven = keep.tile([P, HALF_O, PACK], BF16, name=f"woven{h}", align_bytes=64)
-            nc.vector.tensor_copy(woven[:], hid[:, h].rearrange("p t o -> p o t"))
+            nc.vector.tensor_copy(
+                woven[:].rearrange("p (c i) t -> p c t i", i=PACK),
+                hid[:, h].rearrange("p t (c i) -> p c t i", i=PACK),
+            )
             hq_w = keep.tile([P, HALF_O], U32, name=f"hq_w{h}", align_bytes=64)
             hq_s = keep.tile([P, HALF_O], U8, name=f"hq_s{h}", align_bytes=64)
             nc.vector.quantize_mx(hq_w[:].bitcast(FP8X4), hq_s[:], woven[:].rearrange("p o t -> p (o t)"))

from contextlib import ExitStack

import concourse.mybir as mybir

K, J, R, T, F, O, S, C, N = 512, 512, 512, 2048, 1024, 256, 256, 512, 256
FLOPS = 2 * K * R * J + 2 * R * N * O

F32 = mybir.dt.float32
BF16 = mybir.dt.bfloat16
I32 = mybir.dt.int32
U32 = mybir.dt.uint32
U16 = mybir.dt.uint16
U8 = mybir.dt.uint8
FP8X4 = mybir.dt.float8_e4m3fn_x4
FP4X4 = mybir.dt.float4_e2m1fn_x4
COPY = mybir.ActivationFunctionType.Copy
ALU = mybir.AluOpType

P = 128
PACK = 4
LIST = 16
HALF_J = J // 2
HALF_O = O // 2


def tile_picked_tokens_store_one_doublepost_one_plain_kernel(
    tc, xt_words, xt_scales, wt_words, wt_scales, sa, sb, sd, wb_words, wb_scales,
    offs, offs2, offs3, offs4, offs5, offs6, offs7, out,
):
    nc = tc.nc
    with ExitStack() as ctx:
        keep = ctx.enter_context(tc.tile_pool(name="keep", bufs=1))
        psum = ctx.enter_context(tc.psum_pool(name="psum", bufs=1))

        def load_list(name, src):
            tile = keep.tile(list(src.shape), U16, name=name)
            nc.sync.dma_start(tile[:], src)
            return tile

        def scale_tile(name, width):
            tile = keep.tile([P, width], U8, name=name, tag=name, align_bytes=64)
            nc.vector.memset(tile[:].bitcast(I32), 0)
            return tile

        def load_scales(tile, src):
            for q in range(4):
                nc.sync.dma_start(
                    tile[32 * q : 32 * q + 4, :].bitcast(I32),
                    src[0, 4 * q : 4 * q + 4, :].bitcast(I32),
                )

        def load_row_weights(name, src):
            tile = keep.tile([P, PACK], F32, name=name)
            nc.sync.dma_start(tile[:], src.rearrange("(p t) o -> p (t o)", t=PACK))
            return tile

        wt_s = scale_tile("wt_s", F)
        xt_s = scale_tile("xt_s", T)
        wb_s = scale_tile("wb_s", N)

        list2 = load_list("list2", offs2)
        list1 = load_list("list1", offs)
        load_scales(wt_s, wt_scales)
        wt_w = keep.tile([P, F], U32, name="wt_w", align_bytes=64)
        nc.sync.dma_start(wt_w[:].bitcast(I32), wt_words[0].rearrange("p f t -> p (f t)").bitcast(I32))
        xt_w = keep.tile([P, T], U16, name="xt_w", align_bytes=64)
        nc.sync.dma_start(xt_w[:].bitcast(I32), xt_words[0].bitcast(I32))
        load_scales(xt_s, xt_scales)
        list3 = load_list("list3", offs3)
        sa_t = load_row_weights("sa_t", sa)
        list4 = load_list("list4", offs4)
        sb_t = load_row_weights("sb_t", sb)
        list5 = load_list("list5", offs5)
        list6 = load_list("list6", offs6)
        list7 = load_list("list7", offs7)
        sd_t = load_row_weights("sd_t", sd)
        wb_w = keep.tile([P, 2 * N], U8, name="wb_w", align_bytes=64)
        nc.sync.dma_start(wb_w[:].bitcast(I32), wb_words[0].bitcast(I32))
        load_scales(wb_s, wb_scales)

        wg_s = keep.tile([P, PACK, P], U8, name="wg_s", align_bytes=64)
        wg_w = keep.tile([P, PACK, P], U32, name="wg_w", tag="wg_w", align_bytes=64)
        nc.vector.tensor_copy(wg_s[:].rearrange("p t m -> p m t"), wt_s[:].indirect(list2[:]))
        nc.vector.tensor_copy(wg_w[:].rearrange("p t m -> p m t"), wt_w[:].indirect(list2[:]))

        xg_w = keep.tile([P, J], U16, name="xg_w", align_bytes=64)
        xg_s = keep.tile([P, J], U8, name="xg_s", align_bytes=64)
        nc.vector.tensor_copy(xg_w[:], xt_w[:].indirect(list1[:]))
        for h in range(2):
            cols = slice(h * HALF_J, (h + 1) * HALF_J)
            entries = list1[:, h * HALF_J // LIST : (h + 1) * HALF_J // LIST]
            nc.vector.tensor_copy(xg_s[:, cols], xt_s[:].indirect(entries))

        def first_product(acc, t, cols):
            nc.tensor.matmul_mx(
                acc, lhsT=wg_w[:, t, :].bitcast(FP8X4), lhsT_scale=wg_s[:, t, :],
                rhs=xg_w[:, cols].bitcast(FP4X4), rhs_scale=xg_s[:, cols], start=True, stop=True,
            )

        a = [keep.tile([P, J], F32, name=f"a{t}") for t in range(PACK)]
        for i, (lo, hi) in enumerate([(0, HALF_J), (HALF_J, HALF_J + P), (HALF_J + P, J)]):
            acc = psum.tile([P, hi - lo], F32, name="acc_first", tag=f"bank{i}")
            first_product(acc[:], 0, slice(lo, hi))
            if hi == J:
                nc.vector.tensor_copy(a[0][:, lo:hi], acc[:])
            else:
                nc.scalar.activation(a[0][:, lo:hi], acc[:], COPY)
        for t in range(1, PACK):
            acc = psum.tile([P, J], F32, name=f"acc{t}")
            first_product(acc[:], t, slice(0, J))
            nc.vector.tensor_copy(a[t][:], acc[:])

        g1 = []
        for t in range(PACK):
            h1 = keep.tile([P, S], F32, name="h1", tag="seats")
            h2 = keep.tile([P, S], F32, name="h2")
            pw = keep.tile([P, C], F32, name="pw", tag=("pw_even", "xt_s")[t % 2], align_bytes=64)
            pv = keep.tile([P, C], F32, name="pv", tag=("pv_even", "wg_w")[t % 2], align_bytes=64)
            nc.vector.memset(pw[:].bitcast(I32), 0)
            nc.vector.memset(pv[:].bitcast(I32), 0)
            nc.scalar.activation(h1[:], a[t][:].indirect(list3[:]), COPY, scale=sa_t[:, t : t + 1])
            nc.scalar.activation(h2[:], a[t][:].indirect(list4[:]), COPY, scale=sb_t[:, t : t + 1])
            nc.scalar.activation(pw[:].indirect(list5[:]), h1[:], COPY)
            nc.scalar.activation(pv[:].indirect(list6[:]), h2[:], COPY)
            diff = keep.tile([P, C], F32, name="diff", bufs=2)
            g = keep.tile([P, C], F32, name=f"g1_{t}")
            halves = [slice(0, C // 2), slice(C // 2, C)]
            for cols in halves:
                nc.vector.tensor_tensor(diff[:, cols], pw[:, cols], pv[:, cols], ALU.subtract)
            for cols in halves:
                nc.vector.scalar_tensor_tensor(g[:, cols], diff[:, cols], -1.0, diff[:, cols], ALU.mult, ALU.max)
            g1.append(g)

        hid = keep.tile([P, 2, PACK, HALF_O], BF16, name="hid", tag="seats")
        out_rows = out.rearrange("(b p) o -> p b o", p=P)
        for h in range(2):
            entries = list7[:, h * HALF_O // LIST : (h + 1) * HALF_O // LIST]
            for t in range(PACK):
                nc.scalar.activation(hid[:, h, t, :], g1[t][:].indirect(entries), COPY, scale=sd_t[:, t : t + 1])
            woven = keep.tile([P, HALF_O, PACK], BF16, name=f"woven{h}", align_bytes=64)
            nc.vector.tensor_copy(
                woven[:].rearrange("p (c i) t -> p c t i", i=PACK),
                hid[:, h].rearrange("p t (c i) -> p c t i", i=PACK),
            )
            hq_w = keep.tile([P, HALF_O], U32, name=f"hq_w{h}", align_bytes=64)
            hq_s = keep.tile([P, HALF_O], U8, name=f"hq_s{h}", align_bytes=64)
            nc.vector.quantize_mx(hq_w[:].bitcast(FP8X4), hq_s[:], woven[:].rearrange("p o t -> p (o t)"))
            for b in range(N // P):
                acc = psum.tile([P, HALF_O], F32, name="acc_out", tag=f"bank{2 * h + b}")
                nc.tensor.matmul_mx(
                    acc[:], lhsT=wb_w[:, 2 * P * b : 2 * P * (b + 1)].bitcast(FP4X4),
                    lhsT_scale=wb_s[:, P * b : P * (b + 1)],
                    rhs=hq_w[:].bitcast(FP8X4), rhs_scale=hq_s[:], start=True, stop=True,
                )
                y = keep.tile([P, HALF_O], F32, name=f"y{h}{b}")
                if b == 0:
                    nc.scalar.copy(y[:], acc[:])
                    nc.scalar.dma_start(out_rows[:, b, h * HALF_O : (h + 1) * HALF_O], y[:])
                else:
                    nc.vector.tensor_copy(y[:], acc[:])
                    nc.sync.dma_start(out_rows[:, b, h * HALF_O : (h + 1) * HALF_O], y[:])
